import numpy as np
import ml_dtypes


def mxq(x, axis, fmt="e4m3"):
    dtype, down = {"e4m3": (ml_dtypes.float8_e4m3fn, 7), "e5m2": (ml_dtypes.float8_e5m2, 14)}[fmt]
    v = np.moveaxis(np.asarray(x, np.float32).astype(ml_dtypes.bfloat16).astype(np.float64), axis, -1)
    blocks = v.reshape(v.shape[:-1] + (-1, 32))
    amax = np.abs(blocks).max(-1, keepdims=True)
    byte = np.maximum(np.where(amax > 0, np.frexp(amax)[1] - 1 + 127, 0) - down, 1)
    scale = np.exp2(byte - 127.0)
    codes = (blocks / scale).astype(np.float32).astype(dtype).astype(np.float64)
    return np.moveaxis((codes * scale).reshape(v.shape), -1, axis)


WIDE = False


def mx_kscale(k):
    if not WIDE:
        return np.ones(k)
    levels = np.array([30, -30])
    if k % 512:
        return np.exp2(np.random.permutation(np.resize(levels, k // 32))).repeat(32)
    a = np.empty((k // 512, 16))
    for p in range(k // 512):
        a[p, :8] = np.random.permutation(np.resize(levels, 8))
        for g in range(8):
            far = levels[np.abs(levels - a[p, g]) >= 10]
            a[p, g + 8] = far[np.random.randint(len(far))]
    return np.exp2(a.ravel()).repeat(32)


def f64(x):
    return np.asarray(x).astype(np.float64)


def striped(idx):
    return np.tile(np.asarray(idx).reshape(-1, 16).T, (8, 1)).astype(np.uint16)


def unstriped(offs):
    return offs[:16].T.reshape(-1).astype(np.int64)


E2M1 = np.array([0.0, 0.5, 1.0, 1.5, 2.0, 3.0, 4.0, 6.0, -0.0, -0.5, -1.0, -1.5, -2.0, -3.0, -4.0, -6.0])


def pack_weight(w, fmt):
    k, n = w.shape
    w = f64(np.asarray(w, np.float32).astype(ml_dtypes.bfloat16)).reshape(k // 32, 32, n)
    amax = np.abs(w).max(1)
    if fmt in ("e4m3", "e5m2"):
        byte = np.frexp(amax)[1] - 1 + 127 - (7 if fmt == "e4m3" else 14)
    else:
        mant, ex = np.frexp(amax / 6.0)
        byte = np.where(mant > 0.5, ex, ex - 1) + 127
    byte = np.clip(np.where(amax > 0, byte, 1), 1, 254)
    scaled = (w * np.exp2(127.0 - byte)[:, None, :]).reshape(k, n).astype(np.float32)
    by_word = np.ascontiguousarray(scaled.reshape(k // 512, 128, 4, n).transpose(0, 1, 3, 2))
    if fmt in ("e4m3", "e5m2"):
        words = by_word.astype(ml_dtypes.float8_e4m3fn if fmt == "e4m3" else ml_dtypes.float8_e5m2).view(np.uint8)
    else:
        c = by_word.astype(ml_dtypes.float4_e2m1fn).view(np.uint8) & 0xF
        words = (c[..., 0::2] | (c[..., 1::2] << 4)).reshape(k // 512, 128, 2 * n)
    return np.ascontiguousarray(words), np.ascontiguousarray(byte.astype(np.uint8).reshape(k // 512, 16, n))


def unpack_weight(words, scales, fmt):
    g, _, n = scales.shape
    words = np.ascontiguousarray(words).reshape(g, 128, n, -1)
    if fmt in ("e4m3", "e5m2"):
        vals = words.view(ml_dtypes.float8_e4m3fn if fmt == "e4m3" else ml_dtypes.float8_e5m2).astype(np.float64)
    else:
        nib = np.empty((g, 128, n, 4), np.uint8)
        nib[..., 0::2] = words & 0xF
        nib[..., 1::2] = words >> 4
        vals = E2M1[nib]
    vals = vals * np.repeat(np.exp2(scales.astype(np.float64) - 127.0), 8, axis=1)[..., None]
    return vals.transpose(0, 1, 3, 2).reshape(g * 512, n)


def sigmoid(v):
    return 1.0 / (1.0 + np.exp(-v))


K, T, J, R, C, O, N, L, E = 512, 2048, 256, 512, 512, 256, 256, 512, 1024


def setup_inputs():
    n = np.random.standard_normal
    idx = np.random.permutation(T)[:J]
    idx2 = np.random.permutation(T)[:J]
    idx3 = np.random.permutation(C)[:J]
    idx4 = np.random.permutation(C)[:J]
    idx5 = np.random.permutation(C)[:O]
    idx6 = np.random.permutation(C)[:O]
    idx7 = np.random.permutation(E)[:O]
    fk = mx_kscale(K)
    fr = mx_kscale(R)
    fl = mx_kscale(L)
    xtp = pack_weight(n((K, T)) / fk[:, None], "e2m1")
    wp = pack_weight(n((K, R)) * 1 / np.sqrt(K) * fk[:, None] * fr, "e5m2")
    wbp = pack_weight(n((R, N)) * 1 / np.sqrt(R) / fr[:, None], "e4m3")
    sxp = pack_weight(n((L, O)) / fl[:, None], "e5m2")
    wsp = pack_weight(n((L, N)) * 1 / np.sqrt(L) * fl[:, None], "e4m3")
    return {
        "xt_words": xtp[0],
        "xt_scales": xtp[1],
        "w_words": wp[0],
        "w_scales": wp[1],
        "wb_words": wbp[0],
        "wb_scales": wbp[1],
        "sx_words": sxp[0],
        "sx_scales": sxp[1],
        "ws_words": wsp[0],
        "ws_scales": wsp[1],
        "tz": (n((N, E))).astype(np.float32),
        "so": (np.random.uniform(0.6, 1.6, (N, 1))).astype(np.float32),
        "bo": (np.random.uniform(-1.0, 1.0, (N, 1))).astype(np.float32),
        "offs": striped(idx),
        "offs2": striped(idx2),
        "offs3": striped(idx3),
        "offs4": striped(idx4),
        "offs5": striped(idx5),
        "offs6": striped(idx6),
        "offs7": striped(idx7),
    }


def reference(xt_words, xt_scales, w_words, w_scales, wb_words, wb_scales, sx_words, sx_scales, ws_words, ws_scales, tz, so, bo, offs, offs2, offs3, offs4, offs5, offs6, offs7):
    idx = unstriped(offs)
    idx2 = unstriped(offs2)
    idx3 = unstriped(offs3)
    idx4 = unstriped(offs4)
    idx5 = unstriped(offs5)
    idx6 = unstriped(offs6)
    idx7 = unstriped(offs7)
    xtu = unpack_weight(xt_words, xt_scales, "e2m1")
    wu = unpack_weight(w_words, w_scales, "e5m2")
    wbu = unpack_weight(wb_words, wb_scales, "e4m3")
    sxu = unpack_weight(sx_words, sx_scales, "e5m2")
    wsu = unpack_weight(ws_words, ws_scales, "e4m3")
    xtidxg = xtu[:, idx]
    a = wu.T @ xtidxg
    xtidx2g = xtu[:, idx2]
    b = wu.T @ xtidx2g
    pw = np.zeros((R, C))
    pw[:, idx3] = a
    pv = np.zeros((R, C))
    pv[:, idx4] = b
    hid = np.abs(pw[:, idx5] - pv[:, idx6])
    hidq = mxq(hid, 0, "e5m2")
    p = wbu.T @ hidq + wsu.T @ sxu
    y = p * sigmoid(f64(tz)[:, idx7] * f64(so) + f64(bo))
    return y

@@ -1,0 +1,206 @@
+from contextlib import ExitStack
+
+import concourse.mybir as mybir
+
+K, T, J, R, C, O, N, L, E = 512, 2048, 256, 512, 512, 256, 256, 512, 1024
+FLOPS = 2 * K * R * 2 * J + 2 * R * N * O + 2 * L * N * O
+
+F32 = mybir.dt.float32
+BF16 = mybir.dt.bfloat16
+I32 = mybir.dt.int32
+U32 = mybir.dt.uint32
+U16 = mybir.dt.uint16
+U8 = mybir.dt.uint8
+E2M1 = mybir.dt.float4_e2m1fn_x4
+E5M2 = mybir.dt.float8_e5m2_x4
+E4M3 = mybir.dt.float8_e4m3fn_x4
+ACT = mybir.ActivationFunctionType
+ALU = mybir.AluOpType
+
+P = 128
+PACK = 4
+HALF = O // 2
+N_TILES = N // P
+
+
+def tile_list_tied_twoboards_skip_finalgate_kernel(
+    tc, xt_words, xt_scales, w_words, w_scales, wb_words, wb_scales, sx_words, sx_scales, ws_words, ws_scales,
+    tz, so, bo, offs, offs2, offs3, offs4, offs5, offs6, offs7, out,
+):
+    nc = tc.nc
+
+    with ExitStack() as ctx:
+        sb = ctx.enter_context(tc.tile_pool(name="sb", bufs=1))
+        ps = ctx.enter_context(tc.psum_pool(name="ps", bufs=1))
+
+        def load_list(src, name):
+            lst = sb.tile([P, J // 16], U16, name=name)
+            nc.sync.dma_start(lst[:], src)
+            return lst
+
+        def load_words(queue, src, name):
+            words = sb.tile([P, src.shape[2]], U32, name=name, align_bytes=64)
+            queue.dma_start(words[:].bitcast(I32), src[0].rearrange("p n t -> p (n t)").bitcast(I32))
+            return words
+
+        def load_scale_rows(queue, plane, src):
+            for q in range(4):
+                queue.dma_start(plane[32 * q : 32 * q + 4, :].bitcast(I32), src[0, 4 * q : 4 * q + 4, :].bitcast(I32))
+
+        def load_quadrant(queue, plane, src, q):
+            rows = src[0, 4 * q : 4 * q + 4, :].bitcast(I32)
+            queue.dma_start(
+                plane[32 * q : 32 * q + 32, :].bitcast(I32), rows.unsqueeze(0).broadcast_to([8, 4, rows.shape[1]])
+            )
+
+        xt_plane = sb.tile([P, T], U8, align_bytes=64)
+        w_plane_raw = sb.tile([P, R], U8, align_bytes=64)
+        xt_tab = sb.tile([P, T], U16, align_bytes=64)
+        slope = sb.tile([P, N_TILES], F32)
+        offset = sb.tile([P, N_TILES], F32)
+        tz_tab = [sb.tile([P, E], F32, name=f"tz{c}", tag=f"tz{c}") for c in range(N_TILES)]
+
+        lst_a = load_list(offs, "lst_a")
+        load_quadrant(nc.scalar, w_plane_raw, w_scales, 0)
+        load_quadrant(nc.sync, w_plane_raw, w_scales, 2)
+        load_quadrant(nc.scalar, w_plane_raw, w_scales, 1)
+        load_quadrant(nc.sync, w_plane_raw, w_scales, 3)
+        w_raw = load_words(nc.scalar, w_words, "w_raw")
+        nc.sync.dma_start(xt_tab[:].bitcast(I32), xt_words[0].bitcast(I32))
+        load_quadrant(nc.scalar, xt_plane, xt_scales, 0)
+        load_quadrant(nc.sync, xt_plane, xt_scales, 1)
+        load_quadrant(nc.scalar, xt_plane, xt_scales, 2)
+        lst_b = load_list(offs2, "lst_b")
+        load_quadrant(nc.scalar, xt_plane, xt_scales, 3)
+        with nc.allow_non_contiguous_dma(reason="one value a partition"):
+            nc.sync.dma_start(offset[:], bo.rearrange("(c p) o -> p (c o)", p=P))
+            nc.scalar.dma_start(tz_tab[0][:], tz[0:P, :])
+            read_z = load_list(offs7, "read_z")
+            nc.scalar.dma_start(slope[:], so.rearrange("(c p) o -> p (c o)", p=P))
+        put_a = load_list(offs3, "put_a")
+        put_b = load_list(offs4, "put_b")
+        read_w = load_list(offs5, "read_w")
+        read_v = load_list(offs6, "read_v")
+        nc.sync.dma_start(tz_tab[1][:], tz[P : 2 * P, :])
+        ws_codes = load_words(nc.sync, ws_words, "ws_codes")
+        sx_codes = load_words(nc.sync, sx_words, "sx_codes")
+        wb_codes = load_words(nc.sync, wb_words, "wb_codes")
+        late_planes = sb.tile([P, 3 * N], U8, align_bytes=64)
+        nc.vector.memset(late_planes[:].bitcast(I32), 0)
+        ws_plane = late_planes[:, 0:N]
+        sx_plane = late_planes[:, N : 2 * N]
+        wb_plane = late_planes[:, 2 * N : 3 * N]
+        load_scale_rows(nc.sync, ws_plane, ws_scales)
+        load_scale_rows(nc.sync, sx_plane, sx_scales)
+        load_scale_rows(nc.sync, wb_plane, wb_scales)
+
+        gate = sb.tile([P, N_TILES, O], F32)
+
+        def gate_rows(c):
+            nc.scalar.activation(
+                out=gate[:, c, :], in_=tz_tab[c][:].indirect(read_z[:]), func=ACT.Sigmoid,
+                bias=offset[:, c : c + 1], scale=slope[:, c : c + 1],
+            )
+
+        gate_rows(0)
+
+        w_codes = sb.tile([P, R], U32, align_bytes=64)
+        w_plane = sb.tile([P, R], U8, align_bytes=64)
+        nc.vector.tensor_copy(
+            out=w_plane[:].rearrange("p (t m) -> p m t", t=PACK),
+            in_=w_plane_raw[:].rearrange("p (m t) -> p m t", t=PACK),
+        )
+        nc.vector.tensor_copy(
+            out=w_codes[:].rearrange("p (t m) -> p m t", t=PACK), in_=w_raw[:].rearrange("p (m t) -> p m t", t=PACK)
+        )
+
+        def gather_tokens(lst, name):
+            codes = sb.tile([P, J], U16, name=name + "_codes", align_bytes=64)
+            plane = sb.tile([P, J], U8, name=name + "_plane", align_bytes=64)
+            nc.vector.tensor_copy(out=codes[:], in_=xt_tab[:].indirect(lst[:]))
+            nc.vector.tensor_copy(out=plane[:], in_=xt_plane[:].indirect(lst[:]))
+            return codes, plane
+
+        def first_product(codes, plane, name):
+            banks = []
+            for u in range(2):
+                bank = ps.tile([P, 2, J], F32, name=f"{name}{u}")
+                for v in range(2):
+                    cols = slice((2 * u + v) * P, (2 * u + v + 1) * P)
+                    nc.tensor.matmul_mx(
+                        out=bank[:, v, :], lhsT=w_codes[:, cols].bitcast(E5M2), lhsT_scale=w_plane[:, cols],
+                        rhs=codes[:].bitcast(E2M1), rhs_scale=plane[:], start=True, stop=True,
+                    )
+                banks.append(bank)
+            return banks
+
+        xa_codes, xa_plane = gather_tokens(lst_a, "xa")
+        a_banks = first_product(xa_codes, xa_plane, "a_bank")
+        xb_codes, xb_plane = gather_tokens(lst_b, "xb")
+        b_banks = first_product(xb_codes, xb_plane, "b_bank")
+
+        pw = [sb.tile([P, C], F32, name=f"pw{t}") for t in range(PACK)]
+        pv = [sb.tile([P, C], F32, name=f"pv{t}") for t in range(PACK)]
+        for t in range(PACK):
+            nc.vector.memset(pw[t][:], 0.0)
+            nc.vector.memset(pv[t][:], 0.0)
+
+        a_sb = [sb.tile([P, 2, J], F32, name="a_sb0", tag="tz0"), sb.tile([P, 2, J], F32, name="a_sb1")]
+        b_sb = [sb.tile([P, 2, J], F32, name=f"b_sb{u}") for u in range(2)]
+        picked_w = [sb.tile([P, O], F32, name=f"picked_w{t}") for t in range(PACK)]
+        diff = [sb.tile([P, PACK, HALF], F32, name=f"diff{h}") for h in range(2)]
+        cols_of_half = HALF // 16
+        for t in range(PACK):
+            u, v = divmod(t, 2)
+            if v == 0:
+                nc.scalar.copy(out=a_sb[u][:], in_=a_banks[u][:])
+                nc.vector.tensor_copy(out=b_sb[u][:], in_=b_banks[u][:])
+            nc.scalar.activation(out=pw[t][:].indirect(put_a[:]), in_=a_sb[u][:, v, :], func=ACT.Copy)
+            nc.scalar.activation(out=picked_w[t][:], in_=pw[t][:].indirect(read_w[:]), func=ACT.Copy)
+            nc.vector.tensor_copy(out=pv[t][:].indirect(put_b[:]), in_=b_sb[u][:, v, :])
+            for h in range(2):
+                nc.vector.tensor_tensor(
+                    out=diff[h][:, t, :],
+                    in0=pv[t][:].indirect(read_v[:, h * cols_of_half : (h + 1) * cols_of_half]),
+                    in1=picked_w[t][:, h * HALF : (h + 1) * HALF],
+                    op=ALU.subtract,
+                )
+
+        gate_rows(1)
+
+        out_banks = [ps.tile([P, N_TILES, HALF], F32, name=f"out_bank{h}") for h in range(2)]
+        for h in range(2):
+            reads = slice(h * HALF, (h + 1) * HALF)
+            for c in range(N_TILES):
+                feats = slice(c * P, (c + 1) * P)
+                nc.tensor.matmul_mx(
+                    out=out_banks[h][:, c, :], lhsT=ws_codes[:, feats].bitcast(E4M3), lhsT_scale=ws_plane[:, feats],
+                    rhs=sx_codes[:, reads].bitcast(E5M2), rhs_scale=sx_plane[:, reads], start=(c == 0), stop=False,
+                )
+
+        out_view = out.rearrange("(c p) o -> p c o", p=P)
+        hid = [sb.tile([P, HALF, PACK], BF16, name=f"hid{h}", align_bytes=64) for h in range(2)]
+        for h in range(2):
+            nc.scalar.activation(
+                out=hid[h][:].rearrange("p (g i) t -> p g t i", i=4),
+                in_=diff[h][:].rearrange("p t (g i) -> p g t i", i=4),
+                func=ACT.Abs,
+            )
+        for h in range(2):
+            reads = slice(h * HALF, (h + 1) * HALF)
+            hid_codes = sb.tile([P, HALF], U32, name=f"hid_codes{h}", align_bytes=64)
+            hid_plane = sb.tile([P, HALF], U8, name=f"hid_plane{h}", align_bytes=64)
+            nc.vector.quantize_mx(
+                out=hid_codes[:].bitcast(E5M2), scales=hid_plane[:], in_=hid[h][:].rearrange("p o t -> p (o t)")
+            )
+            for c in range(N_TILES):
+                feats = slice(c * P, (c + 1) * P)
+                nc.tensor.matmul_mx(
+                    out=out_banks[h][:, c, :], lhsT=wb_codes[:, feats].bitcast(E4M3), lhsT_scale=wb_plane[:, feats],
+                    rhs=hid_codes[:].bitcast(E5M2), rhs_scale=hid_plane[:], start=False, stop=(c == N_TILES - 1),
+                )
+        for h in range(2):
+            reads = slice(h * HALF, (h + 1) * HALF)
+            result = sb.tile([P, N_TILES, HALF], F32, name=f"result{h}")
+            nc.vector.tensor_tensor(out=result[:], in0=out_banks[h][:], in1=gate[:, :, reads], op=ALU.mult)
+            nc.sync.dma_start(out_view[:, :, reads], result[:])

@@ -21,6 +21,8 @@ P = 128
 PACK = 4
 HALF = O // 2
 N_TILES = N // P
+A_GROUPS = ((0,), (1, 2), (3,))
+B_GROUPS = ((0, 1), (2, 3))
 
 
 def tile_list_tied_twoboards_skip_finalgate_kernel(
@@ -53,35 +55,33 @@ def tile_list_tied_twoboards_skip_finalgate_kernel(
                 plane[32 * q : 32 * q + 32, :].bitcast(I32), rows.unsqueeze(0).broadcast_to([8, 4, rows.shape[1]])
             )
 
-        xt_plane = sb.tile([P, T], U8, align_bytes=64)
+        xt_plane = sb.tile([P, T], U8, tag="xt_plane", align_bytes=64)
         w_plane_raw = sb.tile([P, R], U8, align_bytes=64)
-        xt_tab = sb.tile([P, T], U16, align_bytes=64)
+        xt_tab = sb.tile([P, T], U16, tag="xt_tab", align_bytes=64)
         slope = sb.tile([P, N_TILES], F32)
         offset = sb.tile([P, N_TILES], F32)
-        tz_tab = [sb.tile([P, E], F32, name=f"tz{c}", tag=f"tz{c}") for c in range(N_TILES)]
+        tz_tab = [sb.tile([P, E], F32, name=f"tz{c}", tag=f"tz{c}", align_bytes=64) for c in range(N_TILES)]
 
-        lst_a = load_list(offs, "lst_a")
-        load_quadrant(nc.scalar, w_plane_raw, w_scales, 0)
-        load_quadrant(nc.sync, w_plane_raw, w_scales, 2)
-        load_quadrant(nc.scalar, w_plane_raw, w_scales, 1)
-        load_quadrant(nc.sync, w_plane_raw, w_scales, 3)
-        w_raw = load_words(nc.scalar, w_words, "w_raw")
+        xt_plane_words = xt_plane[:].bitcast(I32)
+        nc.vector.memset(xt_plane_words[:, 0 : T // 8], 0)
+        nc.gpsimd.memset(xt_plane_words[:, T // 8 : T // 4], 0)
+
+        for q in range(4):
+            load_quadrant(nc.scalar if q % 2 else nc.sync, w_plane_raw, w_scales, q)
         nc.sync.dma_start(xt_tab[:].bitcast(I32), xt_words[0].bitcast(I32))
-        load_quadrant(nc.scalar, xt_plane, xt_scales, 0)
-        load_quadrant(nc.sync, xt_plane, xt_scales, 1)
-        load_quadrant(nc.scalar, xt_plane, xt_scales, 2)
+        lst_a = load_list(offs, "lst_a")
+        w_raw = load_words(nc.sync, w_words, "w_raw")
+        load_scale_rows(nc.sync, xt_plane, xt_scales)
         lst_b = load_list(offs2, "lst_b")
-        load_quadrant(nc.scalar, xt_plane, xt_scales, 3)
-        with nc.allow_non_contiguous_dma(reason="one value a partition"):
-            nc.sync.dma_start(offset[:], bo.rearrange("(c p) o -> p (c o)", p=P))
-            nc.scalar.dma_start(tz_tab[0][:], tz[0:P, :])
-            read_z = load_list(offs7, "read_z")
-            nc.scalar.dma_start(slope[:], so.rearrange("(c p) o -> p (c o)", p=P))
         put_a = load_list(offs3, "put_a")
         put_b = load_list(offs4, "put_b")
         read_w = load_list(offs5, "read_w")
         read_v = load_list(offs6, "read_v")
-        nc.sync.dma_start(tz_tab[1][:], tz[P : 2 * P, :])
+        read_z = load_list(offs7, "read_z")
+        with nc.allow_non_contiguous_dma(reason="one value a partition"):
+            nc.sync.dma_start(slope[:], so.rearrange("(c p) o -> p (c o)", p=P))
+            nc.sync.dma_start(offset[:], bo.rearrange("(c p) o -> p (c o)", p=P))
+        nc.sync.dma_start(tz_tab[0][:], tz[0:P, :])
         ws_codes = load_words(nc.sync, ws_words, "ws_codes")
         sx_codes = load_words(nc.sync, sx_words, "sx_codes")
         wb_codes = load_words(nc.sync, wb_words, "wb_codes")
@@ -93,6 +93,7 @@ def tile_list_tied_twoboards_skip_finalgate_kernel(
         load_scale_rows(nc.sync, ws_plane, ws_scales)
         load_scale_rows(nc.sync, sx_plane, sx_scales)
         load_scale_rows(nc.sync, wb_plane, wb_scales)
+        nc.sync.dma_start(tz_tab[1][:], tz[P : 2 * P, :])
 
         gate = sb.tile([P, N_TILES, O], F32)
 
@@ -102,17 +103,8 @@ def tile_list_tied_twoboards_skip_finalgate_kernel(
                 bias=offset[:, c : c + 1], scale=slope[:, c : c + 1],
             )
 
-        gate_rows(0)
-
         w_codes = sb.tile([P, R], U32, align_bytes=64)
         w_plane = sb.tile([P, R], U8, align_bytes=64)
-        nc.vector.tensor_copy(
-            out=w_plane[:].rearrange("p (t m) -> p m t", t=PACK),
-            in_=w_plane_raw[:].rearrange("p (m t) -> p m t", t=PACK),
-        )
-        nc.vector.tensor_copy(
-            out=w_codes[:].rearrange("p (t m) -> p m t", t=PACK), in_=w_raw[:].rearrange("p (m t) -> p m t", t=PACK)
-        )
 
         def gather_tokens(lst, name):
             codes = sb.tile([P, J], U16, name=name + "_codes", align_bytes=64)
@@ -121,12 +113,12 @@ def tile_list_tied_twoboards_skip_finalgate_kernel(
             nc.vector.tensor_copy(out=plane[:], in_=xt_plane[:].indirect(lst[:]))
             return codes, plane
 
-        def first_product(codes, plane, name):
+        def first_product(codes, plane, groups, name):
             banks = []
-            for u in range(2):
-                bank = ps.tile([P, 2, J], F32, name=f"{name}{u}")
-                for v in range(2):
-                    cols = slice((2 * u + v) * P, (2 * u + v + 1) * P)
+            for group in groups:
+                bank = ps.tile([P, len(group), J], F32, name=f"{name}{group[0]}")
+                for v, t in enumerate(group):
+                    cols = slice(t * P, (t + 1) * P)
                     nc.tensor.matmul_mx(
                         out=bank[:, v, :], lhsT=w_codes[:, cols].bitcast(E5M2), lhsT_scale=w_plane[:, cols],
                         rhs=codes[:].bitcast(E2M1), rhs_scale=plane[:], start=True, stop=True,
@@ -134,39 +126,94 @@ def tile_list_tied_twoboards_skip_finalgate_kernel(
                 banks.append(bank)
             return banks
 
+        nc.vector.tensor_copy(
+            out=w_plane[:].rearrange("p (t m) -> p m t", t=PACK),
+            in_=w_plane_raw[:].rearrange("p (m t) -> p m t", t=PACK),
+        )
+        nc.vector.tensor_copy(
+            out=w_codes[:].rearrange("p (t m) -> p m t", t=PACK), in_=w_raw[:].rearrange("p (m t) -> p m t", t=PACK)
+        )
         xa_codes, xa_plane = gather_tokens(lst_a, "xa")
-        a_banks = first_product(xa_codes, xa_plane, "a_bank")
+        a_banks = first_product(xa_codes, xa_plane, A_GROUPS, "a_bank")
         xb_codes, xb_plane = gather_tokens(lst_b, "xb")
-        b_banks = first_product(xb_codes, xb_plane, "b_bank")
+        b_banks = first_product(xb_codes, xb_plane, B_GROUPS, "b_bank")
 
         pw = [sb.tile([P, C], F32, name=f"pw{t}") for t in range(PACK)]
         pv = [sb.tile([P, C], F32, name=f"pv{t}") for t in range(PACK)]
-        for t in range(PACK):
-            nc.vector.memset(pw[t][:], 0.0)
-            nc.vector.memset(pv[t][:], 0.0)
+        for board in (pw[0], pw[1], pw[3], pw[2], pv[0], pv[1], pv[3], pv[2]):
+            nc.gpsimd.memset(board[:], 0.0)
 
-        a_sb = [sb.tile([P, 2, J], F32, name="a_sb0", tag="tz0"), sb.tile([P, 2, J], F32, name="a_sb1")]
-        b_sb = [sb.tile([P, 2, J], F32, name=f"b_sb{u}") for u in range(2)]
-        picked_w = [sb.tile([P, O], F32, name=f"picked_w{t}") for t in range(PACK)]
+        a_sb = [
+            sb.tile([P, 1, J], F32, name="a_sb0"),
+            sb.tile([P, 2, J], F32, name="a_sb1", tag="xt_plane", align_bytes=64),
+            sb.tile([P, 1, J], F32, name="a_sb3", tag="xt_tab", align_bytes=64),
+        ]
+        b_sb = [sb.tile([P, len(g), J], F32, name=f"b_sb{g[0]}") for g in B_GROUPS]
+        side_w = (a_banks, a_sb, pw, put_a, read_w, A_GROUPS)
+        side_v = (b_banks, b_sb, pv, put_b, read_v, B_GROUPS)
+        picked = [sb.tile([P, O], F32, name=f"picked{t}") for t in range(PACK)]
         diff = [sb.tile([P, PACK, HALF], F32, name=f"diff{h}") for h in range(2)]
         cols_of_half = HALF // 16
-        for t in range(PACK):
-            u, v = divmod(t, 2)
-            if v == 0:
-                nc.scalar.copy(out=a_sb[u][:], in_=a_banks[u][:])
-                nc.vector.tensor_copy(out=b_sb[u][:], in_=b_banks[u][:])
-            nc.scalar.activation(out=pw[t][:].indirect(put_a[:]), in_=a_sb[u][:, v, :], func=ACT.Copy)
-            nc.scalar.activation(out=picked_w[t][:], in_=pw[t][:].indirect(read_w[:]), func=ACT.Copy)
-            nc.vector.tensor_copy(out=pv[t][:].indirect(put_b[:]), in_=b_sb[u][:, v, :])
+
+        def place_of(groups, t):
+            u = [n for n, g in enumerate(groups) if t in g][0]
+            return u, groups[u].index(t)
+
+        def scalar_stage(side, u):
+            nc.scalar.copy(out=side[1][u][:], in_=side[0][u][:])
+
+        def scalar_put(side, t):
+            banks, staged, boards, put, read, groups = side
+            u, v = place_of(groups, t)
+            nc.scalar.activation(out=boards[t][:].indirect(put[:]), in_=staged[u][:, v, :], func=ACT.Copy)
+
+        def scalar_pick(side, t):
+            banks, staged, boards, put, read, groups = side
+            nc.scalar.activation(out=picked[t][:], in_=boards[t][:].indirect(read[:]), func=ACT.Copy)
+
+        def vector_stage(side, u):
+            nc.vector.tensor_copy(out=side[1][u][:], in_=side[0][u][:])
+
+        def vector_put(side, t):
+            banks, staged, boards, put, read, groups = side
+            u, v = place_of(groups, t)
+            nc.vector.tensor_copy(out=boards[t][:].indirect(put[:]), in_=staged[u][:, v, :])
+
+        def vector_pick_and_subtract(side, t):
+            banks, staged, boards, put, read, groups = side
             for h in range(2):
                 nc.vector.tensor_tensor(
                     out=diff[h][:, t, :],
-                    in0=pv[t][:].indirect(read_v[:, h * cols_of_half : (h + 1) * cols_of_half]),
-                    in1=picked_w[t][:, h * HALF : (h + 1) * HALF],
+                    in0=boards[t][:].indirect(read[:, h * cols_of_half : (h + 1) * cols_of_half]),
+                    in1=picked[t][:, h * HALF : (h + 1) * HALF],
                     op=ALU.subtract,
                 )
 
-        gate_rows(1)
+        vector_stage(side_w, 1)
+        vector_stage(side_w, 2)
+
+        scalar_stage(side_w, 0)
+        scalar_put(side_w, 0)
+        scalar_stage(side_v, 0)
+        scalar_pick(side_w, 0)
+        scalar_put(side_w, 3)
+        scalar_stage(side_v, 1)
+        scalar_pick(side_w, 3)
+        scalar_put(side_v, 1)
+        scalar_put(side_v, 2)
+        scalar_pick(side_v, 1)
+        scalar_pick(side_v, 2)
+
+        vector_put(side_w, 1)
+        vector_put(side_w, 2)
+        vector_put(side_v, 0)
+        vector_put(side_v, 3)
+        vector_pick_and_subtract(side_v, 0)
+        vector_pick_and_subtract(side_v, 3)
+        vector_pick_and_subtract(side_w, 1)
+        vector_pick_and_subtract(side_w, 2)
+
+        gate_rows(0)
 
         out_banks = [ps.tile([P, N_TILES, HALF], F32, name=f"out_bank{h}") for h in range(2)]
         for h in range(2):
@@ -179,19 +226,20 @@ def tile_list_tied_twoboards_skip_finalgate_kernel(
                 )
 
         out_view = out.rearrange("(c p) o -> p c o", p=P)
-        hid = [sb.tile([P, HALF, PACK], BF16, name=f"hid{h}", align_bytes=64) for h in range(2)]
+        hid = sb.tile([P, O * PACK], BF16, tag="tz0", align_bytes=64)
         for h in range(2):
             nc.scalar.activation(
-                out=hid[h][:].rearrange("p (g i) t -> p g t i", i=4),
+                out=hid[:, h * HALF * PACK : (h + 1) * HALF * PACK].rearrange("p (g i t) -> p g t i", i=4, t=PACK),
                 in_=diff[h][:].rearrange("p t (g i) -> p g t i", i=4),
                 func=ACT.Abs,
             )
+        gate_rows(1)
         for h in range(2):
             reads = slice(h * HALF, (h + 1) * HALF)
             hid_codes = sb.tile([P, HALF], U32, name=f"hid_codes{h}", align_bytes=64)
             hid_plane = sb.tile([P, HALF], U8, name=f"hid_plane{h}", align_bytes=64)
             nc.vector.quantize_mx(
-                out=hid_codes[:].bitcast(E5M2), scales=hid_plane[:], in_=hid[h][:].rearrange("p o t -> p (o t)")
+                out=hid_codes[:].bitcast(E5M2), scales=hid_plane[:], in_=hid[:, h * HALF * PACK : (h + 1) * HALF * PACK]
             )
             for c in range(N_TILES):
                 feats = slice(c * P, (c + 1) * P)

@@ -62,9 +62,11 @@ def tile_list_tied_twoboards_skip_finalgate_kernel(
         offset = sb.tile([P, N_TILES], F32)
         tz_tab = [sb.tile([P, E], F32, name=f"tz{c}", tag=f"tz{c}", align_bytes=64) for c in range(N_TILES)]
 
-        xt_plane_words = xt_plane[:].bitcast(I32)
-        nc.vector.memset(xt_plane_words[:, 0 : T // 8], 0)
-        nc.gpsimd.memset(xt_plane_words[:, T // 8 : T // 4], 0)
+        nc.vector.memset(xt_plane[:].bitcast(I32), 0)
+        pw = [sb.tile([P, C], F32, name=f"pw{t}") for t in range(PACK)]
+        pv = [sb.tile([P, C], F32, name=f"pv{t}") for t in range(PACK)]
+        for board in pw + pv:
+            nc.vector.memset(board[:], 0.0)
 
         for q in range(4):
             load_quadrant(nc.scalar if q % 2 else nc.sync, w_plane_raw, w_scales, q)
@@ -95,11 +97,14 @@ def tile_list_tied_twoboards_skip_finalgate_kernel(
         load_scale_rows(nc.sync, wb_plane, wb_scales)
         nc.sync.dma_start(tz_tab[1][:], tz[P : 2 * P, :])
 
-        gate = sb.tile([P, N_TILES, O], F32)
+        warm_in = sb.tile([P, 1], F32)
+        warm_out = sb.tile([P, 1], F32)
+        nc.gpsimd.memset(warm_in[:], 0.0)
+        nc.scalar.activation(out=warm_out[:], in_=warm_in[:], func=ACT.Sigmoid)
 
-        def gate_rows(c):
+        def gate_rows(c, gate):
             nc.scalar.activation(
-                out=gate[:, c, :], in_=tz_tab[c][:].indirect(read_z[:]), func=ACT.Sigmoid,
+                out=gate[:], in_=tz_tab[c][:].indirect(read_z[:]), func=ACT.Sigmoid,
                 bias=offset[:, c : c + 1], scale=slope[:, c : c + 1],
             )
 
@@ -138,11 +143,6 @@ def tile_list_tied_twoboards_skip_finalgate_kernel(
         xb_codes, xb_plane = gather_tokens(lst_b, "xb")
         b_banks = first_product(xb_codes, xb_plane, B_GROUPS, "b_bank")
 
-        pw = [sb.tile([P, C], F32, name=f"pw{t}") for t in range(PACK)]
-        pv = [sb.tile([P, C], F32, name=f"pv{t}") for t in range(PACK)]
-        for board in (pw[0], pw[1], pw[3], pw[2], pv[0], pv[1], pv[3], pv[2]):
-            nc.gpsimd.memset(board[:], 0.0)
-
         a_sb = [
             sb.tile([P, 1, J], F32, name="a_sb0"),
             sb.tile([P, 2, J], F32, name="a_sb1", tag="xt_plane", align_bytes=64),
@@ -152,7 +152,7 @@ def tile_list_tied_twoboards_skip_finalgate_kernel(
         side_w = (a_banks, a_sb, pw, put_a, read_w, A_GROUPS)
         side_v = (b_banks, b_sb, pv, put_b, read_v, B_GROUPS)
         picked = [sb.tile([P, O], F32, name=f"picked{t}") for t in range(PACK)]
-        diff = [sb.tile([P, PACK, HALF], F32, name=f"diff{h}") for h in range(2)]
+        diff = [sb.tile([P, PACK, HALF], F32, name=f"diff{h}", tag=f"diff{h}") for h in range(2)]
         cols_of_half = HALF // 16
 
         def place_of(groups, t):
@@ -213,7 +213,8 @@ def tile_list_tied_twoboards_skip_finalgate_kernel(
         vector_pick_and_subtract(side_w, 1)
         vector_pick_and_subtract(side_w, 2)
 
-        gate_rows(0)
+        gates = [sb.tile([P, O], F32, name="gate0"), sb.tile([P, O], F32, name="gate1", tag="diff1")]
+        gate_rows(0, gates[0])
 
         out_banks = [ps.tile([P, N_TILES, HALF], F32, name=f"out_bank{h}") for h in range(2)]
         for h in range(2):
@@ -233,7 +234,7 @@ def tile_list_tied_twoboards_skip_finalgate_kernel(
                 in_=diff[h][:].rearrange("p t (g i) -> p g t i", i=4),
                 func=ACT.Abs,
             )
-        gate_rows(1)
+        gate_rows(1, gates[1])
         for h in range(2):
             reads = slice(h * HALF, (h + 1) * HALF)
             hid_codes = sb.tile([P, HALF], U32, name=f"hid_codes{h}", align_bytes=64)
@@ -250,5 +251,8 @@ def tile_list_tied_twoboards_skip_finalgate_kernel(
         for h in range(2):
             reads = slice(h * HALF, (h + 1) * HALF)
             result = sb.tile([P, N_TILES, HALF], F32, name=f"result{h}")
-            nc.vector.tensor_tensor(out=result[:], in0=out_banks[h][:], in1=gate[:, :, reads], op=ALU.mult)
+            for c in range(N_TILES):
+                nc.vector.tensor_tensor(
+                    out=result[:, c, :], in0=out_banks[h][:, c, :], in1=gates[c][:, reads], op=ALU.mult
+                )
             nc.sync.dma_start(out_view[:, :, reads], result[:])

from contextlib import ExitStack

import concourse.mybir as mybir

K, T, J, R, C, O, N, L, E = 512, 2048, 256, 512, 512, 256, 256, 512, 1024
FLOPS = 2 * K * R * 2 * J + 2 * R * N * O + 2 * L * N * O

F32 = mybir.dt.float32
BF16 = mybir.dt.bfloat16
I32 = mybir.dt.int32
U32 = mybir.dt.uint32
U16 = mybir.dt.uint16
U8 = mybir.dt.uint8
E2M1 = mybir.dt.float4_e2m1fn_x4
E5M2 = mybir.dt.float8_e5m2_x4
E4M3 = mybir.dt.float8_e4m3fn_x4
ACT = mybir.ActivationFunctionType
ALU = mybir.AluOpType

P = 128
PACK = 4
HALF = O // 2
N_TILES = N // P
A_GROUPS = ((0,), (1, 2), (3,))
B_GROUPS = ((0, 1), (2, 3))


def tile_list_tied_twoboards_skip_finalgate_kernel(
    tc, xt_words, xt_scales, w_words, w_scales, wb_words, wb_scales, sx_words, sx_scales, ws_words, ws_scales,
    tz, so, bo, offs, offs2, offs3, offs4, offs5, offs6, offs7, out,
):
    nc = tc.nc

    with ExitStack() as ctx:
        sb = ctx.enter_context(tc.tile_pool(name="sb", bufs=1))
        ps = ctx.enter_context(tc.psum_pool(name="ps", bufs=1))

        def load_list(src, name):
            lst = sb.tile([P, J // 16], U16, name=name)
            nc.sync.dma_start(lst[:], src)
            return lst

        def load_words(queue, src, name):
            words = sb.tile([P, src.shape[2]], U32, name=name, align_bytes=64)
            queue.dma_start(words[:].bitcast(I32), src[0].rearrange("p n t -> p (n t)").bitcast(I32))
            return words

        def load_scale_rows(queue, plane, src):
            for q in range(4):
                queue.dma_start(plane[32 * q : 32 * q + 4, :].bitcast(I32), src[0, 4 * q : 4 * q + 4, :].bitcast(I32))

        def load_quadrant(queue, plane, src, q):
            rows = src[0, 4 * q : 4 * q + 4, :].bitcast(I32)
            queue.dma_start(
                plane[32 * q : 32 * q + 32, :].bitcast(I32), rows.unsqueeze(0).broadcast_to([8, 4, rows.shape[1]])
            )

        xt_plane = sb.tile([P, T], U8, tag="xt_plane", align_bytes=64)
        w_plane_raw = sb.tile([P, R], U8, align_bytes=64)
        xt_tab = sb.tile([P, T], U16, tag="xt_tab", align_bytes=64)
        slope = sb.tile([P, N_TILES], F32)
        offset = sb.tile([P, N_TILES], F32)
        tz_tab = [sb.tile([P, E], F32, name=f"tz{c}", tag=f"tz{c}", align_bytes=64) for c in range(N_TILES)]

        nc.vector.memset(xt_plane[:].bitcast(I32), 0)
        pw = [sb.tile([P, C], F32, name=f"pw{t}") for t in range(PACK)]
        pv = [sb.tile([P, C], F32, name=f"pv{t}") for t in range(PACK)]
        for board in pw + pv:
            nc.vector.memset(board[:], 0.0)

        for q in range(4):
            load_quadrant(nc.scalar if q % 2 else nc.sync, w_plane_raw, w_scales, q)
        nc.sync.dma_start(xt_tab[:].bitcast(I32), xt_words[0].bitcast(I32))
        lst_a = load_list(offs, "lst_a")
        w_raw = load_words(nc.sync, w_words, "w_raw")
        load_scale_rows(nc.sync, xt_plane, xt_scales)
        lst_b = load_list(offs2, "lst_b")
        put_a = load_list(offs3, "put_a")
        put_b = load_list(offs4, "put_b")
        read_w = load_list(offs5, "read_w")
        read_v = load_list(offs6, "read_v")
        read_z = load_list(offs7, "read_z")
        with nc.allow_non_contiguous_dma(reason="one value a partition"):
            nc.sync.dma_start(slope[:], so.rearrange("(c p) o -> p (c o)", p=P))
            nc.sync.dma_start(offset[:], bo.rearrange("(c p) o -> p (c o)", p=P))
        nc.sync.dma_start(tz_tab[0][:], tz[0:P, :])
        ws_codes = load_words(nc.sync, ws_words, "ws_codes")
        sx_codes = load_words(nc.sync, sx_words, "sx_codes")
        wb_codes = load_words(nc.sync, wb_words, "wb_codes")
        late_planes = sb.tile([P, 3 * N], U8, align_bytes=64)
        nc.vector.memset(late_planes[:].bitcast(I32), 0)
        ws_plane = late_planes[:, 0:N]
        sx_plane = late_planes[:, N : 2 * N]
        wb_plane = late_planes[:, 2 * N : 3 * N]
        load_scale_rows(nc.sync, ws_plane, ws_scales)
        load_scale_rows(nc.sync, sx_plane, sx_scales)
        load_scale_rows(nc.sync, wb_plane, wb_scales)
        nc.sync.dma_start(tz_tab[1][:], tz[P : 2 * P, :])

        warm_in = sb.tile([P, 1], F32)
        warm_out = sb.tile([P, 1], F32)
        nc.gpsimd.memset(warm_in[:], 0.0)
        nc.scalar.activation(out=warm_out[:], in_=warm_in[:], func=ACT.Sigmoid)

        def gate_rows(c, gate):
            nc.scalar.activation(
                out=gate[:], in_=tz_tab[c][:].indirect(read_z[:]), func=ACT.Sigmoid,
                bias=offset[:, c : c + 1], scale=slope[:, c : c + 1],
            )

        w_codes = sb.tile([P, R], U32, align_bytes=64)
        w_plane = sb.tile([P, R], U8, align_bytes=64)

        def gather_tokens(lst, name):
            codes = sb.tile([P, J], U16, name=name + "_codes", align_bytes=64)
            plane = sb.tile([P, J], U8, name=name + "_plane", align_bytes=64)
            nc.vector.tensor_copy(out=codes[:], in_=xt_tab[:].indirect(lst[:]))
            nc.vector.tensor_copy(out=plane[:], in_=xt_plane[:].indirect(lst[:]))
            return codes, plane

        def first_product(codes, plane, groups, name):
            banks = []
            for group in groups:
                bank = ps.tile([P, len(group), J], F32, name=f"{name}{group[0]}")
                for v, t in enumerate(group):
                    cols = slice(t * P, (t + 1) * P)
                    nc.tensor.matmul_mx(
                        out=bank[:, v, :], lhsT=w_codes[:, cols].bitcast(E5M2), lhsT_scale=w_plane[:, cols],
                        rhs=codes[:].bitcast(E2M1), rhs_scale=plane[:], start=True, stop=True,
                    )
                banks.append(bank)
            return banks

        nc.vector.tensor_copy(
            out=w_plane[:].rearrange("p (t m) -> p m t", t=PACK),
            in_=w_plane_raw[:].rearrange("p (m t) -> p m t", t=PACK),
        )
        nc.vector.tensor_copy(
            out=w_codes[:].rearrange("p (t m) -> p m t", t=PACK), in_=w_raw[:].rearrange("p (m t) -> p m t", t=PACK)
        )
        xa_codes, xa_plane = gather_tokens(lst_a, "xa")
        a_banks = first_product(xa_codes, xa_plane, A_GROUPS, "a_bank")
        xb_codes, xb_plane = gather_tokens(lst_b, "xb")
        b_banks = first_product(xb_codes, xb_plane, B_GROUPS, "b_bank")

        a_sb = [
            sb.tile([P, 1, J], F32, name="a_sb0"),
            sb.tile([P, 2, J], F32, name="a_sb1", tag="xt_plane", align_bytes=64),
            sb.tile([P, 1, J], F32, name="a_sb3", tag="xt_tab", align_bytes=64),
        ]
        b_sb = [sb.tile([P, len(g), J], F32, name=f"b_sb{g[0]}") for g in B_GROUPS]
        side_w = (a_banks, a_sb, pw, put_a, read_w, A_GROUPS)
        side_v = (b_banks, b_sb, pv, put_b, read_v, B_GROUPS)
        picked = [sb.tile([P, O], F32, name=f"picked{t}") for t in range(PACK)]
        diff = [sb.tile([P, PACK, HALF], F32, name=f"diff{h}", tag=f"diff{h}") for h in range(2)]
        cols_of_half = HALF // 16

        def place_of(groups, t):
            u = [n for n, g in enumerate(groups) if t in g][0]
            return u, groups[u].index(t)

        def scalar_stage(side, u):
            nc.scalar.copy(out=side[1][u][:], in_=side[0][u][:])

        def scalar_put(side, t):
            banks, staged, boards, put, read, groups = side
            u, v = place_of(groups, t)
            nc.scalar.activation(out=boards[t][:].indirect(put[:]), in_=staged[u][:, v, :], func=ACT.Copy)

        def scalar_pick(side, t):
            banks, staged, boards, put, read, groups = side
            nc.scalar.activation(out=picked[t][:], in_=boards[t][:].indirect(read[:]), func=ACT.Copy)

        def vector_stage(side, u):
            nc.vector.tensor_copy(out=side[1][u][:], in_=side[0][u][:])

        def vector_put(side, t):
            banks, staged, boards, put, read, groups = side
            u, v = place_of(groups, t)
            nc.vector.tensor_copy(out=boards[t][:].indirect(put[:]), in_=staged[u][:, v, :])

        def vector_pick_and_subtract(side, t):
            banks, staged, boards, put, read, groups = side
            for h in range(2):
                nc.vector.tensor_tensor(
                    out=diff[h][:, t, :],
                    in0=boards[t][:].indirect(read[:, h * cols_of_half : (h + 1) * cols_of_half]),
                    in1=picked[t][:, h * HALF : (h + 1) * HALF],
                    op=ALU.subtract,
                )

        vector_stage(side_w, 1)
        vector_stage(side_w, 2)

        scalar_stage(side_w, 0)
        scalar_put(side_w, 0)
        scalar_stage(side_v, 0)
        scalar_pick(side_w, 0)
        scalar_put(side_w, 3)
        scalar_stage(side_v, 1)
        scalar_pick(side_w, 3)
        scalar_put(side_v, 1)
        scalar_put(side_v, 2)
        scalar_pick(side_v, 1)
        scalar_pick(side_v, 2)

        vector_put(side_w, 1)
        vector_put(side_w, 2)
        vector_put(side_v, 0)
        vector_put(side_v, 3)
        vector_pick_and_subtract(side_v, 0)
        vector_pick_and_subtract(side_v, 3)
        vector_pick_and_subtract(side_w, 1)
        vector_pick_and_subtract(side_w, 2)

        gates = [sb.tile([P, O], F32, name="gate0"), sb.tile([P, O], F32, name="gate1", tag="diff1")]
        gate_rows(0, gates[0])

        out_banks = [ps.tile([P, N_TILES, HALF], F32, name=f"out_bank{h}") for h in range(2)]
        for h in range(2):
            reads = slice(h * HALF, (h + 1) * HALF)
            for c in range(N_TILES):
                feats = slice(c * P, (c + 1) * P)
                nc.tensor.matmul_mx(
                    out=out_banks[h][:, c, :], lhsT=ws_codes[:, feats].bitcast(E4M3), lhsT_scale=ws_plane[:, feats],
                    rhs=sx_codes[:, reads].bitcast(E5M2), rhs_scale=sx_plane[:, reads], start=(c == 0), stop=False,
                )

        out_view = out.rearrange("(c p) o -> p c o", p=P)
        hid = sb.tile([P, O * PACK], BF16, tag="tz0", align_bytes=64)
        for h in range(2):
            nc.scalar.activation(
                out=hid[:, h * HALF * PACK : (h + 1) * HALF * PACK].rearrange("p (g i t) -> p g t i", i=4, t=PACK),
                in_=diff[h][:].rearrange("p t (g i) -> p g t i", i=4),
                func=ACT.Abs,
            )
        gate_rows(1, gates[1])
        for h in range(2):
            reads = slice(h * HALF, (h + 1) * HALF)
            hid_codes = sb.tile([P, HALF], U32, name=f"hid_codes{h}", align_bytes=64)
            hid_plane = sb.tile([P, HALF], U8, name=f"hid_plane{h}", align_bytes=64)
            nc.vector.quantize_mx(
                out=hid_codes[:].bitcast(E5M2), scales=hid_plane[:], in_=hid[:, h * HALF * PACK : (h + 1) * HALF * PACK]
            )
            for c in range(N_TILES):
                feats = slice(c * P, (c + 1) * P)
                nc.tensor.matmul_mx(
                    out=out_banks[h][:, c, :], lhsT=wb_codes[:, feats].bitcast(E4M3), lhsT_scale=wb_plane[:, feats],
                    rhs=hid_codes[:].bitcast(E5M2), rhs_scale=hid_plane[:], start=False, stop=(c == N_TILES - 1),
                )
        for h in range(2):
            reads = slice(h * HALF, (h + 1) * HALF)
            result = sb.tile([P, N_TILES, HALF], F32, name=f"result{h}")
            for c in range(N_TILES):
                nc.vector.tensor_tensor(
                    out=result[:, c, :], in0=out_banks[h][:, c, :], in1=gates[c][:, reads], op=ALU.mult
                )
            nc.sync.dma_start(out_view[:, :, reads], result[:])
